import numpy as np
import ml_dtypes


def mxq(x, axis, fmt="e4m3"):
    dtype, down = {"e4m3": (ml_dtypes.float8_e4m3fn, 7), "e5m2": (ml_dtypes.float8_e5m2, 14)}[fmt]
    v = np.moveaxis(np.asarray(x, np.float32).astype(ml_dtypes.bfloat16).astype(np.float64), axis, -1)
    blocks = v.reshape(v.shape[:-1] + (-1, 32))
    amax = np.abs(blocks).max(-1, keepdims=True)
    byte = np.maximum(np.where(amax > 0, np.frexp(amax)[1] - 1 + 127, 0) - down, 1)
    scale = np.exp2(byte - 127.0)
    codes = (blocks / scale).astype(np.float32).astype(dtype).astype(np.float64)
    return np.moveaxis((codes * scale).reshape(v.shape), -1, axis)


WIDE = False


def mx_kscale(k):
    if not WIDE:
        return np.ones(k)
    levels = np.array([10, -10, 5, -5, 0])
    if k % 512:
        return np.exp2(np.random.permutation(np.resize(levels, k // 32))).repeat(32)
    a = np.empty((k // 512, 16))
    for p in range(k // 512):
        a[p, :8] = np.random.permutation(np.resize(levels, 8))
        for g in range(8):
            far = levels[np.abs(levels - a[p, g]) >= 10]
            a[p, g + 8] = far[np.random.randint(len(far))]
    return np.exp2(a.ravel()).repeat(32)


def f64(x):
    return np.asarray(x).astype(np.float64)


def striped(idx):
    return np.tile(idx.reshape(-1, 16).T, (8, 1)).astype(np.uint16)


def unstriped(offs):
    return offs[:16].T.reshape(-1).astype(np.int64)


E2M1 = np.array([0.0, 0.5, 1.0, 1.5, 2.0, 3.0, 4.0, 6.0, -0.0, -0.5, -1.0, -1.5, -2.0, -3.0, -4.0, -6.0])


def pack_weight(w, fmt):
    k, n = w.shape
    w = f64(np.asarray(w, np.float32).astype(ml_dtypes.bfloat16)).reshape(k // 32, 32, n)
    amax = np.abs(w).max(1)
    if fmt == "e4m3":
        byte = np.frexp(amax)[1] - 1 + 127 - 7
    else:
        mant, ex = np.frexp(amax / 6.0)
        byte = np.where(mant > 0.5, ex, ex - 1) + 127
    byte = np.clip(np.where(amax > 0, byte, 1), 1, 254)
    scaled = (w * np.exp2(127.0 - byte)[:, None, :]).reshape(k, n).astype(np.float32)
    by_word = np.ascontiguousarray(scaled.reshape(k // 512, 128, 4, n).transpose(0, 1, 3, 2))
    if fmt == "e4m3":
        words = by_word.astype(ml_dtypes.float8_e4m3fn).view(np.uint8)
    else:
        c = by_word.astype(ml_dtypes.float4_e2m1fn).view(np.uint8) & 0xF
        words = (c[..., 0::2] | (c[..., 1::2] << 4)).reshape(k // 512, 128, 2 * n)
    return np.ascontiguousarray(words), np.ascontiguousarray(byte.astype(np.uint8).reshape(k // 512, 16, n))


def unpack_weight(words, scales, fmt):
    g, _, n = scales.shape
    words = np.ascontiguousarray(words).reshape(g, 128, n, -1)
    if fmt == "e4m3":
        vals = words.view(ml_dtypes.float8_e4m3fn).astype(np.float64)
    else:
        nib = np.empty((g, 128, n, 4), np.uint8)
        nib[..., 0::2] = words & 0xF
        nib[..., 1::2] = words >> 4
        vals = E2M1[nib]
    vals = vals * np.repeat(np.exp2(scales.astype(np.float64) - 127.0), 8, axis=1)[..., None]
    return vals.transpose(0, 1, 3, 2).reshape(g * 512, n)


def gelu(v):
    return 0.5 * v * (1.0 + np.tanh(np.sqrt(2.0 / np.pi) * (v + 0.044715 * v**3)))


def bf(x):
    return np.asarray(x, np.float32).astype(ml_dtypes.bfloat16)


def planes(Y):
    n, m = Y.shape
    b = f64(bf(Y)).reshape(n // 32, 32, m)
    amax = np.abs(b).max(1)
    byte = np.clip(np.where(amax > 0, np.frexp(amax)[1] - 1 + 127 - 7, 1), 1, 254)
    codes = (b * np.exp2(127.0 - byte)[:, None, :]).reshape(n, m).astype(np.float32).astype(ml_dtypes.float8_e4m3fn).view(np.uint8)
    words = codes.reshape(n // 512, 128, 4, m).transpose(0, 1, 3, 2)
    return np.ascontiguousarray(words), np.ascontiguousarray(byte.astype(np.uint8).reshape(n // 512, 16, m))


K, K2, T, TB, S, P, H, N = 1536, 1024, 4096, 2048, 1024, 512, 512, 1024

def setup_inputs():
    n = np.random.standard_normal
    s = mx_kscale(K)[:, None]
    s2 = mx_kscale(K2)[:, None]
    u = mx_kscale(H)[:, None]
    d = {}
    d["tab_words"], d["tab_scales"] = pack_weight(n((K, T)) * s, "e4m3")
    d["tab2_words"], d["tab2_scales"] = pack_weight(n((K2, TB)) * s2, "e4m3")
    d["offs"] = striped(np.random.permutation(T)[:S])
    d["offs2"] = striped(np.random.permutation(TB)[:P])
    d["pos1"] = striped(np.random.permutation(S)[:P])
    d["wa_words"], d["wa_scales"] = pack_weight(0.43 * n((K, H)) / K**0.5 / s, "e2m1")
    d["wb"] = (0.58 * n((K2, H)) / K2**0.5 / s2).astype(np.float32)
    d["wgs"] = np.exp(0.3 * n((128, P))).astype(np.float32)
    d["gain"] = (np.exp(0.3 * n(H)) * u[:, 0]).astype(np.float32)
    d["w2"] = (n((H, N)) / H**0.5 / u * np.exp(0.8 * n(N))[None, :]).astype(np.float32)
    return d

def reference(tab_words, tab_scales, tab2_words, tab2_scales, offs, offs2, pos1,
              wa_words, wa_scales, wb, wgs, gain, w2):
    v = unpack_weight(tab_words, tab_scales, "e4m3")[:, unstriped(offs)]
    v2 = unpack_weight(tab2_words, tab2_scales, "e4m3")[:, unstriped(offs2)]
    wa = unpack_weight(wa_words, wa_scales, "e2m1")
    a = wa.T @ v
    b = np.sin(mxq(f64(wb), 0, "e4m3").T @ v2)
    placed = np.zeros((H, S))
    placed[:, unstriped(pos1)] = np.tile(f64(wgs), (H // 128, 1)) * b
    z = (np.tanh(a + placed) + a) * f64(gain)[:, None]
    y = mxq(f64(w2), 0, "e4m3").T @ mxq(z, 0, "e4m3")
    words, scales = planes(y)
    return y, words, scales

@@ -1,0 +1,350 @@
+import math
+from contextlib import ExitStack
+
+import concourse.mybir as mybir
+from concourse.masks import make_identity
+
+K, K2, T, TB, S, L, H, N = 1536, 1024, 4096, 2048, 1024, 512, 512, 1024
+FLOPS = 2 * (K * H * S + K2 * H * L + H * N * S)
+
+F32 = mybir.dt.float32
+BF16 = mybir.dt.bfloat16
+I32 = mybir.dt.int32
+U32 = mybir.dt.uint32
+U16 = mybir.dt.uint16
+U8 = mybir.dt.uint8
+FP8X4 = mybir.dt.float8_e4m3fn_x4
+FP4X4 = mybir.dt.float4_e2m1fn_x4
+ALU = mybir.AluOpType
+ACT = mybir.ActivationFunctionType
+
+P = 128
+PA = K // 512
+PB = K2 // 512
+G = N // 512
+HALF = 512
+CHUNK = 256
+ON_SCALAR = ()
+ROUNDER = 1.5 * 2.0**23
+PER_TURN = 1.0 / (2.0 * math.pi)
+
+
+def tile_list_milk_bottle_features_kernel(
+    tc, tab_words, tab_scales, tab2_words, tab2_scales, offs, offs2, pos1,
+    wa_words, wa_scales, wb, wgs, gain, w2, out_0, out_1, out_2,
+):
+    nc = tc.nc
+    with ExitStack() as ctx:
+        held = ctx.enter_context(tc.tile_pool(name="held", bufs=1))
+        ring = ctx.enter_context(tc.tile_pool(name="ring", bufs=2))
+        psum = ctx.enter_context(tc.psum_pool(name="psum", bufs=1))
+
+        def words_of(packed, a):
+            return packed[a].rearrange("p n i -> p (n i)").bitcast(I32)
+
+        tab2_sc = held.tile([P, TB], U8, align_bytes=64)
+        tab_sc = held.tile([P, T], U8, align_bytes=64)
+        wa_sc_raw = held.tile([P, PA, H], U8, align_bytes=64)
+        v_sc_moved = [held.tile([P, S], U8, name=f"v_sc_moved{a}", align_bytes=64) for a in range(1, PA)]
+        pages = [held.tile([P, S], F32, name=f"page{t}") for t in range(4)]
+        nc.vector.memset(tab_sc[:].bitcast(I32), 0)
+        nc.gpsimd.memset(tab2_sc[:].bitcast(I32), 0)
+        nc.vector.memset(wa_sc_raw[:].bitcast(I32), 0)
+        for moved in v_sc_moved:
+            nc.vector.memset(moved[:].bitcast(I32), 0)
+        warm = held.tile([P, 2], F32)
+        nc.gpsimd.memset(warm[:, 0:1], 0.0)
+        nc.scalar.activation(warm[:, 1:2], warm[:, 0:1], ACT.Silu)
+        for q in range(4):
+            (nc.gpsimd, nc.scalar)[q % 2].dma_start(
+                out=tab_sc[32 * q : 32 * q + 4 * PA, :].bitcast(I32),
+                in_=tab_scales[:, 4 * q : 4 * q + 4, :].bitcast(I32),
+            )
+        for q in range(4):
+            nc.gpsimd.dma_start(
+                out=wa_sc_raw[32 * q : 32 * q + 4, :, :].bitcast(I32),
+                in_=wa_scales[:, 4 * q : 4 * q + 4, :].rearrange("a r c -> r a c").bitcast(I32),
+            )
+        ident = held.tile([P, P], F32)
+        make_identity(nc, ident[:])
+        for t in range(4):
+            nc.gpsimd.memset(pages[t][:], 0.0)
+        gain_sb = held.tile([P, 4], F32)
+
+        offs2_sb = held.tile([P, L // 16], U16)
+        offs_sb = held.tile([P, S // 16], U16)
+        pos_sb = held.tile([P, L // 16], U16)
+        tab2_w = [
+            held.tile([P, TB], I32, name=f"tab2_w{a}", tag=("tab2_w0", "tab_w2")[a], align_bytes=64) for a in range(PB)
+        ]
+        wb_raw = [
+            held.tile([P, 4, H], F32, name=f"wb_raw{a}", tag=("raw", "tab_w1")[a], align_bytes=64) for a in range(PB)
+        ]
+        tab_w = {0: held.tile([P, T], I32, name="tab_w0", tag="tab_w0", align_bytes=64)}
+        wgs_sb = held.tile([P, 4, L], F32)
+        wa_raw = held.tile([P, PA, 2 * H], U8, align_bytes=64)
+        wb_rows = wb.rearrange("(a p i) r -> a p i r", a=PB, i=4)
+
+        nc.sync.dma_start(out=wa_raw[:].bitcast(I32), in_=wa_words.rearrange("a p c -> p a c").bitcast(I32))
+        nc.sync.dma_start(offs2_sb[:], offs2)
+        nc.sync.dma_start(offs_sb[:], offs)
+        nc.sync.dma_start(out=wb_raw[0][:], in_=wb_rows[0])
+        for q in range(4):
+            nc.sync.dma_start(
+                out=tab2_sc[32 * q : 32 * q + 4 * PB, :].bitcast(I32),
+                in_=tab2_scales[:, 4 * q : 4 * q + 4, :].bitcast(I32),
+            )
+        nc.sync.dma_start(out=wb_raw[1][:], in_=wb_rows[1])
+        for a in range(PB):
+            nc.sync.dma_start(out=tab2_w[a][:], in_=words_of(tab2_words, a))
+        nc.sync.dma_start(pos_sb[:], pos1)
+        for q in range(4):
+            nc.sync.dma_start(out=wgs_sb[32 * q : 32 * (q + 1)], in_=wgs.rearrange("(p t) l -> p t l", t=4))
+        nc.sync.dma_start(out=tab_w[0][:], in_=words_of(tab_words, 0))
+        nc.sync.dma_start(out=gain_sb[:], in_=gain.rearrange("(p t) -> p t", t=4))
+
+        wa_w = held.tile([P, PA, 4, P, 2], U8, align_bytes=64)
+        nc.vector.tensor_copy(out=wa_w[:], in_=wa_raw[:].rearrange("p a (m t b) -> p a t m b", t=4, b=2))
+        wa_sc = held.tile([P, PA, 4, P], U8, align_bytes=64)
+        nc.vector.tensor_copy(out=wa_sc[:], in_=wa_sc_raw[:].rearrange("p a (m t) -> p a t m", t=4))
+
+        def quantise_weight(raw, staged, name):
+            codes = held.tile([P, 512], U32, name=f"{name}_q", align_bytes=64)
+            scales = held.tile([P, 512], U8, name=f"{name}_sc", align_bytes=64)
+            nc.scalar.copy(
+                out=staged[:].rearrange("p t m i -> p m t i"), in_=raw[:].rearrange("p i (m t) -> p m t i", t=4)
+            )
+            nc.vector.quantize_mx(
+                out=codes[:].bitcast(FP8X4), scales=scales[:], in_=staged[:].rearrange("p t m i -> p (t m i)")
+            )
+            return codes, scales
+
+        wb_q = []
+        for a in range(PB):
+            wb_bf = ring.tile([P, 4, P, 4], BF16, align_bytes=64)
+            wb_q.append(quantise_weight(wb_raw[a], wb_bf, f"wb{a}"))
+
+        v2_w = [held.tile([P, L], U32, name=f"v2_w{a}", align_bytes=64) for a in range(PB)]
+        v2_sc = held.tile([P, L], U8, align_bytes=64)
+        nc.vector.tensor_copy(v2_sc[:], tab2_sc[:].indirect(offs2_sb[:]))
+        nc.vector.tensor_copy(v2_w[0][:], tab2_w[0][:].bitcast(U32).indirect(offs2_sb[:]))
+        for h in range(2):
+            nc.vector.tensor_copy(
+                v2_w[1][:, 256 * h : 256 * (h + 1)],
+                tab2_w[1][:].bitcast(U32).indirect(offs2_sb[:, 16 * h : 16 * (h + 1)]),
+            )
+
+        v_sc0 = held.tile([P, S], U8, align_bytes=64)
+        nc.vector.tensor_copy(v_sc0[:], tab_sc[:].indirect(offs_sb[:]))
+        for a in range(1, PA):
+            nc.gpsimd.dma_start(
+                out=v_sc_moved[a - 1][0:112, :].bitcast(I32), in_=v_sc0[4 * a : 4 * a + 112, :].bitcast(I32)
+            )
+        v_sc = [v_sc0] + v_sc_moved
+
+        w2_raw = [
+            held.tile([P, 4, 512], F32, name=f"w2_raw{g}", tag=("w2_raw0", "raw")[g], align_bytes=64) for g in range(G)
+        ]
+        w2_rows = w2.rearrange("(p i) n -> p i n", i=4)
+        for g in range(G):
+            nc.sync.dma_start(out=w2_raw[g][:], in_=w2_rows[:, :, 512 * g : 512 * (g + 1)])
+        for a in range(1, PA):
+            tab_w[a] = held.tile([P, T], I32, name=f"tab_w{a}", tag=f"tab_w{a}", align_bytes=64)
+            nc.sync.dma_start(out=tab_w[a][:], in_=words_of(tab_words, a))
+
+        def reduce_angle(bank, t, l0, width):
+            entries = slice(l0, l0 + width)
+            x = psum.tile([P, width], F32, tag=bank, bufs=(4 if bank == "y" else 1))
+            for a in range(PB):
+                codes, scales = wb_q[a]
+                nc.tensor.matmul_mx(
+                    out=x[:],
+                    lhsT=codes[:, P * t : P * (t + 1)].bitcast(FP8X4),
+                    lhsT_scale=scales[:, P * t : P * (t + 1)],
+                    rhs=v2_w[a][:, entries].bitcast(FP8X4),
+                    rhs_scale=v2_sc[4 * a : P, entries],
+                    start=(a == 0),
+                    stop=(a == PB - 1),
+                )
+            shifted = ring.tile([P, width], U32)
+            nc.scalar.activation(shifted[:], x[:], ACT.Copy, bias=ROUNDER, scale=PER_TURN)
+            whole = ring.tile([P, width], F32)
+            frac = ring.tile([P, width], F32)
+            nc.scalar.activation(whole[:], shifted[:], ACT.Copy, bias=-ROUNDER)
+            nc.vector.scalar_tensor_tensor(frac[:], x[:], PER_TURN, whole[:], ALU.mult, ALU.subtract)
+            return frac
+
+        def split_angle(t):
+            x = psum.tile([P, 4, P], F32, tag=("a0" if t == 3 else "y"), bufs=(1 if t == 3 else 4))
+            for lb in range(4):
+                entries = slice(P * lb, P * (lb + 1))
+                for a in range(PB):
+                    codes, scales = wb_q[a]
+                    nc.tensor.matmul_mx(
+                        out=x[:, lb, :],
+                        lhsT=v2_w[a][:, entries].bitcast(FP8X4),
+                        lhsT_scale=v2_sc[4 * a : P, entries],
+                        rhs=codes[:, P * t : P * (t + 1)].bitcast(FP8X4),
+                        rhs_scale=scales[:, P * t : P * (t + 1)],
+                        start=(a == 0),
+                        stop=(a == PB - 1),
+                    )
+            shifted = ring.tile([P, 4, P], U32)
+            nc.scalar.activation(shifted[:], x[:], ACT.Copy, bias=ROUNDER, scale=PER_TURN)
+            if t < 3:
+                turns = ring.tile([P, 4, P], F32)
+                whole = ring.tile([P, 4, P], F32)
+            else:
+                turns = held.tile([P, 4, P], F32, tag="w2_bf0", align_bytes=64)
+                whole = held.tile([P, 4, P], F32, tag="w2_bf1", align_bytes=64)
+            nc.scalar.activation(turns[:], x[:], ACT.Copy, scale=PER_TURN)
+            nc.scalar.activation(whole[:], shifted[:], ACT.Copy, bias=ROUNDER, scale=-1.0)
+            frac = psum.tile([P, L], F32, tag=f"a{t}", bufs=1)
+            for lb in range(4):
+                nc.tensor.matmul(
+                    frac[:, P * lb : P * (lb + 1)], turns[:, lb, :], ident[:], start=(lb == 0), stop=False, is_transpose=True
+                )
+            for lb in range(4):
+                nc.tensor.matmul(
+                    frac[:, P * lb : P * (lb + 1)], whole[:, lb, :], ident[:], start=False, stop=(lb == 3), is_transpose=True
+                )
+            return frac
+
+        def place(t, frac, l0, width):
+            b = held.tile([P, width], F32, tag=f"sine{t}_{l0}", align_bytes=64)
+            nc.scalar.activation(b[:], frac[:], ACT.Sin, scale=2.0 * math.pi)
+            nc.vector.tensor_tensor(
+                pages[t][:].indirect(pos_sb[:, l0 // 16 : (l0 + width) // 16]),
+                b[:],
+                wgs_sb[:, t, l0 : l0 + width],
+                ALU.mult,
+            )
+
+        for h in range(2):
+            place(0, reduce_angle("y", 0, h * L // 2, L // 2), h * L // 2, L // 2)
+        fracs = {1: split_angle(1)}
+        for t in range(1, 4):
+            if t < 3:
+                fracs[t + 1] = split_angle(t + 1)
+            place(t, fracs[t], 0, L)
+
+        v_w = [held.tile([P, S], U32, name=f"v_w{a}", tag=("sine0_256", "sine2_0", "sine3_0")[a], align_bytes=64) for a in range(PA)]
+        for a in range(PA - 1):
+            nc.vector.tensor_copy(v_w[a][:], tab_w[a][:].bitcast(U32).indirect(offs_sb[:]))
+
+        w2_q = []
+        for g in range(G):
+            w2_bf = held.tile([P, 4, P, 4], BF16, tag=f"w2_bf{g}", align_bytes=64)
+            w2_q.append(quantise_weight(w2_raw[g], w2_bf, f"w2{g}"))
+
+        y_q = held.tile([P, G, S], U32, align_bytes=64)
+        y_sc = held.tile([P, G, S], U8, align_bytes=64)
+        y_rows = out_0.rearrange("(g p t) j -> g p t j", g=G, t=4)
+        y_words = out_1.rearrange("g p m i -> p g (m i)").bitcast(I32)
+
+        def gather_last(h):
+            nc.vector.tensor_copy(
+                v_w[PA - 1][:, HALF * h : HALF * (h + 1)],
+                tab_w[PA - 1][:].bitcast(U32).indirect(offs_sb[:, 32 * h : 32 * (h + 1)]),
+            )
+
+        def make_a(h):
+            cols = slice(HALF * h, HALF * (h + 1))
+            banks = []
+            for t in range(4):
+                acc = psum.tile([P, HALF], F32, tag=f"a{t}", bufs=1)
+                for a in range(PA):
+                    nc.tensor.matmul_mx(
+                        out=acc[:],
+                        lhsT=wa_w[:, a, t].rearrange("p m b -> p (m b)").bitcast(FP4X4),
+                        lhsT_scale=wa_sc[:, a, t, :],
+                        rhs=v_w[a][:, cols].bitcast(FP8X4),
+                        rhs_scale=v_sc[a][:, cols],
+                        start=(a == 0),
+                        stop=(a == PA - 1),
+                    )
+                banks.append(acc)
+            return banks
+
+        def make_z(c, banks):
+            cols = slice(CHUNK * c, CHUNK * (c + 1))
+            z_rows = ring.tile([P, 4, CHUNK], BF16, align_bytes=64)
+            for t in range(4):
+                acc = banks[t][:, CHUNK * (c % 2) : CHUNK * (c % 2 + 1)]
+                s = ring.tile([P, CHUNK], F32, bufs=4)
+                nc.vector.tensor_tensor(s[:], acc, pages[t][:, cols], ALU.add)
+                a_gain = ring.tile([P, CHUNK], F32, bufs=4)
+                nc.scalar.activation(a_gain[:], acc, ACT.Copy, scale=gain_sb[:, t : t + 1])
+                th = ring.tile([P, CHUNK], F32, bufs=4)
+                nc.scalar.activation(th[:], s[:], ACT.Tanh)
+                nc.vector.scalar_tensor_tensor(
+                    z_rows[:, t, :], th[:], gain_sb[:, t : t + 1], a_gain[:], ALU.mult, ALU.add
+                )
+            z_bf = ring.tile([P, CHUNK, 4], BF16, align_bytes=64)
+            interleave = nc.scalar.copy if c in ON_SCALAR else nc.vector.tensor_copy
+            interleave(
+                out=z_bf[:].rearrange("p (c e) t -> p c t e", e=4),
+                in_=z_rows[:].rearrange("p t (c e) -> p c t e", e=4),
+            )
+            z_q = ring.tile([P, CHUNK], U32, align_bytes=64)
+            z_sc = ring.tile([P, CHUNK], U8, align_bytes=64)
+            nc.vector.quantize_mx(out=z_q[:].bitcast(FP8X4), scales=z_sc[:], in_=z_bf[:].rearrange("p j t -> p (j t)"))
+            return z_q, z_sc
+
+        def make_y(c, z_q, z_sc):
+            cols = slice(CHUNK * c, CHUNK * (c + 1))
+            y_both = held.tile([P, G, 4, CHUNK], F32, tag=("tab_w0", "tab_w1", "raw", "w2_raw0")[c], align_bytes=64)
+            for g in range(G):
+                codes, scales = w2_q[g]
+                y_sb = y_both[:, g]
+                for tt in range(2):
+                    bank = psum.tile([P, 2, CHUNK], F32, tag="y", bufs=4)
+                    for e in range(2):
+                        t = 2 * tt + e
+                        nc.tensor.matmul_mx(
+                            out=bank[:, e, :],
+                            lhsT=codes[:, P * t : P * (t + 1)].bitcast(FP8X4),
+                            lhsT_scale=scales[:, P * t : P * (t + 1)],
+                            rhs=z_q[:].bitcast(FP8X4),
+                            rhs_scale=z_sc[:],
+                            start=True,
+                            stop=True,
+                        )
+                    nc.scalar.copy(out=y_sb[:, 2 * tt : 2 * tt + 2, :], in_=bank[:])
+                nc.sync.dma_start(out=y_rows[g][:, :, cols], in_=y_sb)
+            return y_both
+
+        def make_planes(c, y_both):
+            cols = slice(CHUNK * c, CHUNK * (c + 1))
+            for g in range(G):
+                y_sb = y_both[:, g]
+                y_bf = ring.tile([P, CHUNK, 4], BF16, align_bytes=64)
+                nc.vector.tensor_copy(
+                    out=y_bf[:].rearrange("p (c e) t -> p c t e", e=4),
+                    in_=y_sb.rearrange("p t (c e) -> p c t e", e=4),
+                )
+                nc.vector.quantize_mx(
+                    out=y_q[:, g, cols].bitcast(FP8X4), scales=y_sc[:, g, cols], in_=y_bf[:].rearrange("p j t -> p (j t)")
+                )
+            nc.sync.dma_start(out=y_words[:, :, cols], in_=y_q[:, :, cols].bitcast(I32))
+
+        gather_last(0)
+        banks = make_a(0)
+        z_planes = {0: make_z(0, banks)}
+        gather_last(1)
+        y_chunks = {}
+        for c in range(S // CHUNK):
+            y_chunks[c] = make_y(c, *z_planes[c])
+            if c == 1:
+                banks = make_a(1)
+            if c + 1 < S // CHUNK:
+                z_planes[c + 1] = make_z(c + 1, banks)
+            if c > 0:
+                make_planes(c - 1, y_chunks[c - 1])
+        make_planes(S // CHUNK - 1, y_chunks[S // CHUNK - 1])
+
+        for q in range(4):
+            nc.sync.dma_start(
+                out=out_2[:, 4 * q : 4 * q + 4, :].rearrange("g r m -> r g m").bitcast(I32),
+                in_=y_sc[32 * q : 32 * q + 4, :, :].bitcast(I32),
+            )

@@ -25,6 +25,7 @@ G = N // 512
 HALF = 512
 CHUNK = 256
 ON_SCALAR = ()
+Y_ON_SCALAR = ()
 ROUNDER = 1.5 * 2.0**23
 PER_TURN = 1.0 / (2.0 * math.pi)
 
@@ -47,24 +48,14 @@ def tile_list_milk_bottle_features_kernel(
         wa_sc_raw = held.tile([P, PA, H], U8, align_bytes=64)
         v_sc_moved = [held.tile([P, S], U8, name=f"v_sc_moved{a}", align_bytes=64) for a in range(1, PA)]
         pages = [held.tile([P, S], F32, name=f"page{t}") for t in range(4)]
-        nc.vector.memset(tab_sc[:].bitcast(I32), 0)
-        nc.gpsimd.memset(tab2_sc[:].bitcast(I32), 0)
+        nc.vector.memset(tab2_sc[:].bitcast(I32), 0)
         nc.vector.memset(wa_sc_raw[:].bitcast(I32), 0)
+        nc.vector.memset(tab_sc[:].bitcast(I32), 0)
         for moved in v_sc_moved:
             nc.vector.memset(moved[:].bitcast(I32), 0)
         warm = held.tile([P, 2], F32)
         nc.gpsimd.memset(warm[:, 0:1], 0.0)
         nc.scalar.activation(warm[:, 1:2], warm[:, 0:1], ACT.Silu)
-        for q in range(4):
-            (nc.gpsimd, nc.scalar)[q % 2].dma_start(
-                out=tab_sc[32 * q : 32 * q + 4 * PA, :].bitcast(I32),
-                in_=tab_scales[:, 4 * q : 4 * q + 4, :].bitcast(I32),
-            )
-        for q in range(4):
-            nc.gpsimd.dma_start(
-                out=wa_sc_raw[32 * q : 32 * q + 4, :, :].bitcast(I32),
-                in_=wa_scales[:, 4 * q : 4 * q + 4, :].rearrange("a r c -> r a c").bitcast(I32),
-            )
         ident = held.tile([P, P], F32)
         make_identity(nc, ident[:])
         for t in range(4):
@@ -75,7 +66,7 @@ def tile_list_milk_bottle_features_kernel(
         offs_sb = held.tile([P, S // 16], U16)
         pos_sb = held.tile([P, L // 16], U16)
         tab2_w = [
-            held.tile([P, TB], I32, name=f"tab2_w{a}", tag=("tab2_w0", "tab_w2")[a], align_bytes=64) for a in range(PB)
+            held.tile([P, TB], I32, name=f"tab2_w{a}", tag=("tab_w2", "tab2_w1")[a], align_bytes=64) for a in range(PB)
         ]
         wb_raw = [
             held.tile([P, 4, H], F32, name=f"wb_raw{a}", tag=("raw", "tab_w1")[a], align_bytes=64) for a in range(PB)
@@ -87,7 +78,6 @@ def tile_list_milk_bottle_features_kernel(
 
         nc.sync.dma_start(out=wa_raw[:].bitcast(I32), in_=wa_words.rearrange("a p c -> p a c").bitcast(I32))
         nc.sync.dma_start(offs2_sb[:], offs2)
-        nc.sync.dma_start(offs_sb[:], offs)
         nc.sync.dma_start(out=wb_raw[0][:], in_=wb_rows[0])
         for q in range(4):
             nc.sync.dma_start(
@@ -95,8 +85,19 @@ def tile_list_milk_bottle_features_kernel(
                 in_=tab2_scales[:, 4 * q : 4 * q + 4, :].bitcast(I32),
             )
         nc.sync.dma_start(out=wb_raw[1][:], in_=wb_rows[1])
+        for q in range(4):
+            nc.sync.dma_start(
+                out=wa_sc_raw[32 * q : 32 * q + 4, :, :].bitcast(I32),
+                in_=wa_scales[:, 4 * q : 4 * q + 4, :].rearrange("a r c -> r a c").bitcast(I32),
+            )
         for a in range(PB):
             nc.sync.dma_start(out=tab2_w[a][:], in_=words_of(tab2_words, a))
+        nc.sync.dma_start(offs_sb[:], offs)
+        for q in range(4):
+            nc.sync.dma_start(
+                out=tab_sc[32 * q : 32 * q + 4 * PA, :].bitcast(I32),
+                in_=tab_scales[:, 4 * q : 4 * q + 4, :].bitcast(I32),
+            )
         nc.sync.dma_start(pos_sb[:], pos1)
         for q in range(4):
             nc.sync.dma_start(out=wgs_sb[32 * q : 32 * (q + 1)], in_=wgs.rearrange("(p t) l -> p t l", t=4))
@@ -134,12 +135,8 @@ def tile_list_milk_bottle_features_kernel(
                 tab2_w[1][:].bitcast(U32).indirect(offs2_sb[:, 16 * h : 16 * (h + 1)]),
             )
 
-        v_sc0 = held.tile([P, S], U8, align_bytes=64)
+        v_sc0 = held.tile([P, S], U8, tag="tab2_w1", align_bytes=64)
         nc.vector.tensor_copy(v_sc0[:], tab_sc[:].indirect(offs_sb[:]))
-        for a in range(1, PA):
-            nc.gpsimd.dma_start(
-                out=v_sc_moved[a - 1][0:112, :].bitcast(I32), in_=v_sc0[4 * a : 4 * a + 112, :].bitcast(I32)
-            )
         v_sc = [v_sc0] + v_sc_moved
 
         w2_raw = [
@@ -148,6 +145,10 @@ def tile_list_milk_bottle_features_kernel(
         w2_rows = w2.rearrange("(p i) n -> p i n", i=4)
         for g in range(G):
             nc.sync.dma_start(out=w2_raw[g][:], in_=w2_rows[:, :, 512 * g : 512 * (g + 1)])
+        for a in range(1, PA):
+            nc.sync.dma_start(
+                out=v_sc_moved[a - 1][0:112, :].bitcast(I32), in_=v_sc0[4 * a : 4 * a + 112, :].bitcast(I32)
+            )
         for a in range(1, PA):
             tab_w[a] = held.tile([P, T], I32, name=f"tab_w{a}", tag=f"tab_w{a}", align_bytes=64)
             nc.sync.dma_start(out=tab_w[a][:], in_=words_of(tab_words, a))
@@ -169,7 +170,7 @@ def tile_list_milk_bottle_features_kernel(
             shifted = ring.tile([P, width], U32)
             nc.scalar.activation(shifted[:], x[:], ACT.Copy, bias=ROUNDER, scale=PER_TURN)
             whole = ring.tile([P, width], F32)
-            frac = ring.tile([P, width], F32)
+            frac = held.tile([P, width], F32, tag=f"first{l0}")
             nc.scalar.activation(whole[:], shifted[:], ACT.Copy, bias=-ROUNDER)
             nc.vector.scalar_tensor_tensor(frac[:], x[:], PER_TURN, whole[:], ALU.mult, ALU.subtract)
             return frac
@@ -189,7 +190,7 @@ def tile_list_milk_bottle_features_kernel(
                         start=(a == 0),
                         stop=(a == PB - 1),
                     )
-            shifted = ring.tile([P, 4, P], U32)
+            shifted = held.tile([P, 4, P], U32, tag=("first0", "first256")[t % 2 - 1])
             nc.scalar.activation(shifted[:], x[:], ACT.Copy, bias=ROUNDER, scale=PER_TURN)
             if t < 3:
                 turns = ring.tile([P, 4, P], F32)
@@ -286,8 +287,8 @@ def tile_list_milk_bottle_features_kernel(
                 out=z_bf[:].rearrange("p (c e) t -> p c t e", e=4),
                 in_=z_rows[:].rearrange("p t (c e) -> p c t e", e=4),
             )
-            z_q = ring.tile([P, CHUNK], U32, align_bytes=64)
-            z_sc = ring.tile([P, CHUNK], U8, align_bytes=64)
+            z_q = ring.tile([P, CHUNK], U32, bufs=4, align_bytes=64)
+            z_sc = ring.tile([P, CHUNK], U8, bufs=4, align_bytes=64)
             nc.vector.quantize_mx(out=z_q[:].bitcast(FP8X4), scales=z_sc[:], in_=z_bf[:].rearrange("p j t -> p (j t)"))
             return z_q, z_sc
 
@@ -318,8 +319,9 @@ def tile_list_milk_bottle_features_kernel(
             cols = slice(CHUNK * c, CHUNK * (c + 1))
             for g in range(G):
                 y_sb = y_both[:, g]
-                y_bf = ring.tile([P, CHUNK, 4], BF16, align_bytes=64)
-                nc.vector.tensor_copy(
+                y_bf = ring.tile([P, CHUNK, 4], BF16, bufs=3, align_bytes=64)
+                interleave = nc.scalar.copy if (c, g) in Y_ON_SCALAR else nc.vector.tensor_copy
+                interleave(
                     out=y_bf[:].rearrange("p (c e) t -> p c t e", e=4),
                     in_=y_sb.rearrange("p t (c e) -> p c t e", e=4),
                 )
@@ -329,19 +331,23 @@ def tile_list_milk_bottle_features_kernel(
             nc.sync.dma_start(out=y_words[:, :, cols], in_=y_q[:, :, cols].bitcast(I32))
 
         gather_last(0)
-        banks = make_a(0)
-        z_planes = {0: make_z(0, banks)}
+        banks = {0: make_a(0)}
+        z = {}
+        y = {}
+        z[0] = make_z(0, banks[0])
         gather_last(1)
-        y_chunks = {}
-        for c in range(S // CHUNK):
-            y_chunks[c] = make_y(c, *z_planes[c])
-            if c == 1:
-                banks = make_a(1)
-            if c + 1 < S // CHUNK:
-                z_planes[c + 1] = make_z(c + 1, banks)
-            if c > 0:
-                make_planes(c - 1, y_chunks[c - 1])
-        make_planes(S // CHUNK - 1, y_chunks[S // CHUNK - 1])
+        z[1] = make_z(1, banks[0])
+        banks[1] = make_a(1)
+        z[2] = make_z(2, banks[1])
+        y[0] = make_y(0, *z[0])
+        z[3] = make_z(3, banks[1])
+        y[1] = make_y(1, *z[1])
+        y[2] = make_y(2, *z[2])
+        y[3] = make_y(3, *z[3])
+        make_planes(0, y[0])
+        make_planes(1, y[1])
+        make_planes(2, y[2])
+        make_planes(3, y[3])
 
         for q in range(4):
             nc.sync.dma_start(

@@ -43,23 +43,22 @@ def tile_list_milk_bottle_features_kernel(
         def words_of(packed, a):
             return packed[a].rearrange("p n i -> p (n i)").bitcast(I32)
 
-        tab2_sc = held.tile([P, TB], U8, align_bytes=64)
+        tab2_sc = held.tile([P, PB, TB], U8, align_bytes=64)
         tab_sc = held.tile([P, T], U8, align_bytes=64)
         wa_sc_raw = held.tile([P, PA, H], U8, align_bytes=64)
-        v_sc_moved = [held.tile([P, S], U8, name=f"v_sc_moved{a}", align_bytes=64) for a in range(1, PA)]
-        pages = [held.tile([P, S], F32, name=f"page{t}") for t in range(4)]
-        nc.vector.memset(tab2_sc[:].bitcast(I32), 0)
+        v_sc = held.tile([P, PA, S], U8, align_bytes=64)
+        pages = {0: held.tile([P, S], F32, name="page0")}
+        nc.vector.memset(tab2_sc[:, 0, :].bitcast(I32), 0)
+        nc.gpsimd.memset(tab2_sc[:, 1, :].bitcast(I32), 0)
         nc.vector.memset(wa_sc_raw[:].bitcast(I32), 0)
         nc.vector.memset(tab_sc[:].bitcast(I32), 0)
-        for moved in v_sc_moved:
-            nc.vector.memset(moved[:].bitcast(I32), 0)
+        nc.vector.memset(pages[0][:], 0.0)
+        nc.vector.memset(v_sc[:].bitcast(I32), 0)
         warm = held.tile([P, 2], F32)
         nc.gpsimd.memset(warm[:, 0:1], 0.0)
         nc.scalar.activation(warm[:, 1:2], warm[:, 0:1], ACT.Silu)
         ident = held.tile([P, P], F32)
         make_identity(nc, ident[:])
-        for t in range(4):
-            nc.gpsimd.memset(pages[t][:], 0.0)
         gain_sb = held.tile([P, 4], F32)
 
         offs2_sb = held.tile([P, L // 16], U16)
@@ -78,11 +77,16 @@ def tile_list_milk_bottle_features_kernel(
 
         nc.sync.dma_start(out=wa_raw[:].bitcast(I32), in_=wa_words.rearrange("a p c -> p a c").bitcast(I32))
         nc.sync.dma_start(offs2_sb[:], offs2)
+        nc.sync.dma_start(offs_sb[:], offs)
+        nc.sync.dma_start(pos_sb[:], pos1)
+        nc.sync.dma_start(out=gain_sb[:], in_=gain.rearrange("(p t) -> p t", t=4))
+        wgs_raw = held.tile([P, L], F32)
+        nc.sync.dma_start(out=wgs_raw[:], in_=wgs)
         nc.sync.dma_start(out=wb_raw[0][:], in_=wb_rows[0])
         for q in range(4):
             nc.sync.dma_start(
-                out=tab2_sc[32 * q : 32 * q + 4 * PB, :].bitcast(I32),
-                in_=tab2_scales[:, 4 * q : 4 * q + 4, :].bitcast(I32),
+                out=tab2_sc[32 * q : 32 * q + 4, :, :].bitcast(I32),
+                in_=tab2_scales[:, 4 * q : 4 * q + 4, :].rearrange("a r c -> r a c").bitcast(I32),
             )
         nc.sync.dma_start(out=wb_raw[1][:], in_=wb_rows[1])
         for q in range(4):
@@ -92,20 +96,13 @@ def tile_list_milk_bottle_features_kernel(
             )
         for a in range(PB):
             nc.sync.dma_start(out=tab2_w[a][:], in_=words_of(tab2_words, a))
-        nc.sync.dma_start(offs_sb[:], offs)
-        for q in range(4):
-            nc.sync.dma_start(
-                out=tab_sc[32 * q : 32 * q + 4 * PA, :].bitcast(I32),
-                in_=tab_scales[:, 4 * q : 4 * q + 4, :].bitcast(I32),
-            )
-        nc.sync.dma_start(pos_sb[:], pos1)
-        for q in range(4):
-            nc.sync.dma_start(out=wgs_sb[32 * q : 32 * (q + 1)], in_=wgs.rearrange("(p t) l -> p t l", t=4))
+        nc.sync.dma_start(
+            out=tab_sc[0 : 16 * PA, :].bitcast(I32), in_=tab_scales.rearrange("a q c -> (a q) c").bitcast(I32)
+        )
         nc.sync.dma_start(out=tab_w[0][:], in_=words_of(tab_words, 0))
-        nc.sync.dma_start(out=gain_sb[:], in_=gain.rearrange("(p t) -> p t", t=4))
 
-        wa_w = held.tile([P, PA, 4, P, 2], U8, align_bytes=64)
-        nc.vector.tensor_copy(out=wa_w[:], in_=wa_raw[:].rearrange("p a (m t b) -> p a t m b", t=4, b=2))
+        wa_w = held.tile([P, PA, 4, 2 * P], U8, align_bytes=64)
+        nc.vector.tensor_copy(out=wa_w[:].bitcast(U16), in_=wa_raw[:].bitcast(U16).rearrange("p a (m t) -> p a t m", t=4))
         wa_sc = held.tile([P, PA, 4, P], U8, align_bytes=64)
         nc.vector.tensor_copy(out=wa_sc[:], in_=wa_sc_raw[:].rearrange("p a (m t) -> p a t m", t=4))
 
@@ -120,14 +117,30 @@ def tile_list_milk_bottle_features_kernel(
             )
             return codes, scales
 
+        wgs_turned = psum.tile([P, 4, P], F32, tag="a0", bufs=1)
+        for lb in range(4):
+            nc.tensor.transpose(wgs_turned[:, lb, :], wgs_raw[:, P * lb : P * (lb + 1)], ident[:])
+
+        def deal_wgs(t):
+            repeated = ring.tile([P, 4, 4, 32], F32)
+            rows = wgs_turned[:].rearrange("l b (q t) -> l b t q", t=4)[:, :, t, :]
+            nc.scalar.copy(out=repeated[:], in_=rows.unsqueeze(2).to_broadcast([P, 4, 4, 32]))
+            dealt = psum.tile([P, 4, P], F32, tag=f"a{1 + t % 3}", bufs=1)
+            for lb in range(4):
+                nc.tensor.transpose(dealt[:, lb, :], repeated[:, lb].rearrange("l e q -> l (e q)"), ident[:])
+            nc.scalar.copy(out=wgs_sb[:, t, :], in_=dealt[:].rearrange("p b l -> p (b l)"))
+
+        deal_wgs(0)
         wb_q = []
         for a in range(PB):
             wb_bf = ring.tile([P, 4, P, 4], BF16, align_bytes=64)
             wb_q.append(quantise_weight(wb_raw[a], wb_bf, f"wb{a}"))
+        deal_wgs(1)
 
         v2_w = [held.tile([P, L], U32, name=f"v2_w{a}", align_bytes=64) for a in range(PB)]
-        v2_sc = held.tile([P, L], U8, align_bytes=64)
-        nc.vector.tensor_copy(v2_sc[:], tab2_sc[:].indirect(offs2_sb[:]))
+        v2_sc = held.tile([P, PB, L], U8, align_bytes=64)
+        for a in range(PB):
+            nc.vector.tensor_copy(v2_sc[:, a, :], tab2_sc[:, a, :].indirect(offs2_sb[:]))
         nc.vector.tensor_copy(v2_w[0][:], tab2_w[0][:].bitcast(U32).indirect(offs2_sb[:]))
         for h in range(2):
             nc.vector.tensor_copy(
@@ -137,7 +150,6 @@ def tile_list_milk_bottle_features_kernel(
 
         v_sc0 = held.tile([P, S], U8, tag="tab2_w1", align_bytes=64)
         nc.vector.tensor_copy(v_sc0[:], tab_sc[:].indirect(offs_sb[:]))
-        v_sc = [v_sc0] + v_sc_moved
 
         w2_raw = [
             held.tile([P, 4, 512], F32, name=f"w2_raw{g}", tag=("w2_raw0", "raw")[g], align_bytes=64) for g in range(G)
@@ -146,12 +158,14 @@ def tile_list_milk_bottle_features_kernel(
         for g in range(G):
             nc.sync.dma_start(out=w2_raw[g][:], in_=w2_rows[:, :, 512 * g : 512 * (g + 1)])
         for a in range(1, PA):
-            nc.sync.dma_start(
-                out=v_sc_moved[a - 1][0:112, :].bitcast(I32), in_=v_sc0[4 * a : 4 * a + 112, :].bitcast(I32)
-            )
-        for a in range(1, PA):
             tab_w[a] = held.tile([P, T], I32, name=f"tab_w{a}", tag=f"tab_w{a}", align_bytes=64)
             nc.sync.dma_start(out=tab_w[a][:], in_=words_of(tab_words, a))
+        for a in range(PA):
+            for q in range(4):
+                nc.sync.dma_start(
+                    out=v_sc[32 * q : 32 * q + 4, a, :].bitcast(I32),
+                    in_=v_sc0[16 * a + 4 * q : 16 * a + 4 * q + 4, :].bitcast(I32),
+                )
 
         def reduce_angle(bank, t, l0, width):
             entries = slice(l0, l0 + width)
@@ -163,20 +177,20 @@ def tile_list_milk_bottle_features_kernel(
                     lhsT=codes[:, P * t : P * (t + 1)].bitcast(FP8X4),
                     lhsT_scale=scales[:, P * t : P * (t + 1)],
                     rhs=v2_w[a][:, entries].bitcast(FP8X4),
-                    rhs_scale=v2_sc[4 * a : P, entries],
+                    rhs_scale=v2_sc[:, a, entries],
                     start=(a == 0),
                     stop=(a == PB - 1),
                 )
             shifted = ring.tile([P, width], U32)
             nc.scalar.activation(shifted[:], x[:], ACT.Copy, bias=ROUNDER, scale=PER_TURN)
-            whole = ring.tile([P, width], F32)
+            whole = held.tile([P, width], F32, tag=f"page{1 + l0 // width}")
             frac = held.tile([P, width], F32, tag=f"first{l0}")
             nc.scalar.activation(whole[:], shifted[:], ACT.Copy, bias=-ROUNDER)
             nc.vector.scalar_tensor_tensor(frac[:], x[:], PER_TURN, whole[:], ALU.mult, ALU.subtract)
             return frac
 
         def split_angle(t):
-            x = psum.tile([P, 4, P], F32, tag=("a0" if t == 3 else "y"), bufs=(1 if t == 3 else 4))
+            x = psum.tile([P, 4, P], F32, tag="y", bufs=4)
             for lb in range(4):
                 entries = slice(P * lb, P * (lb + 1))
                 for a in range(PB):
@@ -184,7 +198,7 @@ def tile_list_milk_bottle_features_kernel(
                     nc.tensor.matmul_mx(
                         out=x[:, lb, :],
                         lhsT=v2_w[a][:, entries].bitcast(FP8X4),
-                        lhsT_scale=v2_sc[4 * a : P, entries],
+                        lhsT_scale=v2_sc[:, a, entries],
                         rhs=codes[:, P * t : P * (t + 1)].bitcast(FP8X4),
                         rhs_scale=scales[:, P * t : P * (t + 1)],
                         start=(a == 0),
@@ -223,6 +237,11 @@ def tile_list_milk_bottle_features_kernel(
 
         for h in range(2):
             place(0, reduce_angle("y", 0, h * L // 2, L // 2), h * L // 2, L // 2)
+        for t in range(1, 4):
+            pages[t] = held.tile([P, S], F32, name=f"page{t}", tag=("page1", "page2", "sine0_0")[t - 1], align_bytes=(64 if t == 3 else None))
+            nc.gpsimd.memset(pages[t][:], 0.0)
+        deal_wgs(2)
+        deal_wgs(3)
         fracs = {1: split_angle(1)}
         for t in range(1, 4):
             if t < 3:
@@ -254,14 +273,14 @@ def tile_list_milk_bottle_features_kernel(
             banks = []
             for t in range(4):
                 acc = psum.tile([P, HALF], F32, tag=f"a{t}", bufs=1)
-                for a in range(PA):
+                for a in (1, 0, 2):
                     nc.tensor.matmul_mx(
                         out=acc[:],
-                        lhsT=wa_w[:, a, t].rearrange("p m b -> p (m b)").bitcast(FP4X4),
+                        lhsT=wa_w[:, a, t, :].bitcast(FP4X4),
                         lhsT_scale=wa_sc[:, a, t, :],
                         rhs=v_w[a][:, cols].bitcast(FP8X4),
-                        rhs_scale=v_sc[a][:, cols],
-                        start=(a == 0),
+                        rhs_scale=v_sc[:, a, cols],
+                        start=(a == 1),
                         stop=(a == PA - 1),
                     )
                 banks.append(acc)
@@ -338,10 +357,10 @@ def tile_list_milk_bottle_features_kernel(
         gather_last(1)
         z[1] = make_z(1, banks[0])
         banks[1] = make_a(1)
-        z[2] = make_z(2, banks[1])
         y[0] = make_y(0, *z[0])
-        z[3] = make_z(3, banks[1])
+        z[2] = make_z(2, banks[1])
         y[1] = make_y(1, *z[1])
+        z[3] = make_z(3, banks[1])
         y[2] = make_y(2, *z[2])
         y[3] = make_y(3, *z[3])
         make_planes(0, y[0])

@@ -50,8 +50,8 @@ def tile_list_milk_bottle_features_kernel(
         pages = {0: held.tile([P, S], F32, name="page0")}
         nc.vector.memset(tab2_sc[:, 0, :].bitcast(I32), 0)
         nc.gpsimd.memset(tab2_sc[:, 1, :].bitcast(I32), 0)
-        nc.vector.memset(wa_sc_raw[:].bitcast(I32), 0)
         nc.vector.memset(tab_sc[:].bitcast(I32), 0)
+        nc.vector.memset(wa_sc_raw[:].bitcast(I32), 0)
         nc.vector.memset(pages[0][:], 0.0)
         nc.vector.memset(v_sc[:].bitcast(I32), 0)
         warm = held.tile([P, 2], F32)
@@ -65,7 +65,7 @@ def tile_list_milk_bottle_features_kernel(
         offs_sb = held.tile([P, S // 16], U16)
         pos_sb = held.tile([P, L // 16], U16)
         tab2_w = [
-            held.tile([P, TB], I32, name=f"tab2_w{a}", tag=("tab_w2", "tab2_w1")[a], align_bytes=64) for a in range(PB)
+            held.tile([P, TB], I32, name=f"tab2_w{a}", tag=("tab2_w0", "tab_w2")[a], align_bytes=64) for a in range(PB)
         ]
         wb_raw = [
             held.tile([P, 4, H], F32, name=f"wb_raw{a}", tag=("raw", "tab_w1")[a], align_bytes=64) for a in range(PB)
@@ -75,20 +75,21 @@ def tile_list_milk_bottle_features_kernel(
         wa_raw = held.tile([P, PA, 2 * H], U8, align_bytes=64)
         wb_rows = wb.rearrange("(a p i) r -> a p i r", a=PB, i=4)
 
-        nc.sync.dma_start(out=wa_raw[:].bitcast(I32), in_=wa_words.rearrange("a p c -> p a c").bitcast(I32))
-        nc.sync.dma_start(offs2_sb[:], offs2)
-        nc.sync.dma_start(offs_sb[:], offs)
-        nc.sync.dma_start(pos_sb[:], pos1)
-        nc.sync.dma_start(out=gain_sb[:], in_=gain.rearrange("(p t) -> p t", t=4))
         wgs_raw = held.tile([P, L], F32)
         nc.sync.dma_start(out=wgs_raw[:], in_=wgs)
-        nc.sync.dma_start(out=wb_raw[0][:], in_=wb_rows[0])
+        nc.sync.dma_start(offs2_sb[:], offs2)
         for q in range(4):
             nc.sync.dma_start(
                 out=tab2_sc[32 * q : 32 * q + 4, :, :].bitcast(I32),
                 in_=tab2_scales[:, 4 * q : 4 * q + 4, :].rearrange("a r c -> r a c").bitcast(I32),
             )
+        nc.sync.dma_start(offs_sb[:], offs)
+        nc.sync.dma_start(out=wb_raw[0][:], in_=wb_rows[0])
+        nc.sync.dma_start(
+            out=tab_sc[0 : 16 * PA, :].bitcast(I32), in_=tab_scales.rearrange("a q c -> (a q) c").bitcast(I32)
+        )
         nc.sync.dma_start(out=wb_raw[1][:], in_=wb_rows[1])
+        nc.sync.dma_start(out=wa_raw[:].bitcast(I32), in_=wa_words.rearrange("a p c -> p a c").bitcast(I32))
         for q in range(4):
             nc.sync.dma_start(
                 out=wa_sc_raw[32 * q : 32 * q + 4, :, :].bitcast(I32),
@@ -96,9 +97,8 @@ def tile_list_milk_bottle_features_kernel(
             )
         for a in range(PB):
             nc.sync.dma_start(out=tab2_w[a][:], in_=words_of(tab2_words, a))
-        nc.sync.dma_start(
-            out=tab_sc[0 : 16 * PA, :].bitcast(I32), in_=tab_scales.rearrange("a q c -> (a q) c").bitcast(I32)
-        )
+        nc.sync.dma_start(pos_sb[:], pos1)
+        nc.sync.dma_start(out=gain_sb[:], in_=gain.rearrange("(p t) -> p t", t=4))
         nc.sync.dma_start(out=tab_w[0][:], in_=words_of(tab_words, 0))
 
         wa_w = held.tile([P, PA, 4, 2 * P], U8, align_bytes=64)
@@ -107,7 +107,7 @@ def tile_list_milk_bottle_features_kernel(
         nc.vector.tensor_copy(out=wa_sc[:], in_=wa_sc_raw[:].rearrange("p a (m t) -> p a t m", t=4))
 
         def quantise_weight(raw, staged, name):
-            codes = held.tile([P, 512], U32, name=f"{name}_q", align_bytes=64)
+            codes = held.tile([P, 512], U32, name=f"{name}_q", tag=f"{name}_q", align_bytes=64)
             scales = held.tile([P, 512], U8, name=f"{name}_sc", align_bytes=64)
             nc.scalar.copy(
                 out=staged[:].rearrange("p t m i -> p m t i"), in_=raw[:].rearrange("p i (m t) -> p m t i", t=4)
@@ -122,25 +122,31 @@ def tile_list_milk_bottle_features_kernel(
             nc.tensor.transpose(wgs_turned[:, lb, :], wgs_raw[:, P * lb : P * (lb + 1)], ident[:])
 
         def deal_wgs(t):
-            repeated = ring.tile([P, 4, 4, 32], F32)
+            repeated = spread[t]
             rows = wgs_turned[:].rearrange("l b (q t) -> l b t q", t=4)[:, :, t, :]
-            nc.scalar.copy(out=repeated[:], in_=rows.unsqueeze(2).to_broadcast([P, 4, 4, 32]))
+            nc.scalar.copy(out=repeated, in_=rows.unsqueeze(2).to_broadcast([P, 4, 4, 32]))
             dealt = psum.tile([P, 4, P], F32, tag=f"a{1 + t % 3}", bufs=1)
             for lb in range(4):
                 nc.tensor.transpose(dealt[:, lb, :], repeated[:, lb].rearrange("l e q -> l (e q)"), ident[:])
             nc.scalar.copy(out=wgs_sb[:, t, :], in_=dealt[:].rearrange("p b l -> p (b l)"))
 
+        first_spread = held.tile([P, 2, 4, 4, 32], F32)
+        spread = {t: first_spread[:, t] for t in range(2)}
         deal_wgs(0)
-        wb_q = []
-        for a in range(PB):
-            wb_bf = ring.tile([P, 4, P, 4], BF16, align_bytes=64)
-            wb_q.append(quantise_weight(wb_raw[a], wb_bf, f"wb{a}"))
         deal_wgs(1)
-
-        v2_w = [held.tile([P, L], U32, name=f"v2_w{a}", align_bytes=64) for a in range(PB)]
         v2_sc = held.tile([P, PB, L], U8, align_bytes=64)
         for a in range(PB):
             nc.vector.tensor_copy(v2_sc[:, a, :], tab2_sc[:, a, :].indirect(offs2_sb[:]))
+        wb_q = []
+        for a in range(PB):
+            wb_bf = held.tile([P, 4, P, 4], BF16, name=f"wb_bf{a}", align_bytes=64)
+            wb_q.append(quantise_weight(wb_raw[a], wb_bf, f"wb{a}"))
+        later_spread = held.tile([P, 2, 4, 4, 32], F32, tag="tab_w1", align_bytes=64)
+        for t in range(2, 4):
+            spread[t] = later_spread[:, t - 2]
+            deal_wgs(t)
+
+        v2_w = [held.tile([P, L], U32, name=f"v2_w{a}", align_bytes=64) for a in range(PB)]
         nc.vector.tensor_copy(v2_w[0][:], tab2_w[0][:].bitcast(U32).indirect(offs2_sb[:]))
         for h in range(2):
             nc.vector.tensor_copy(
@@ -148,7 +154,7 @@ def tile_list_milk_bottle_features_kernel(
                 tab2_w[1][:].bitcast(U32).indirect(offs2_sb[:, 16 * h : 16 * (h + 1)]),
             )
 
-        v_sc0 = held.tile([P, S], U8, tag="tab2_w1", align_bytes=64)
+        v_sc0 = held.tile([P, S], U8, align_bytes=64)
         nc.vector.tensor_copy(v_sc0[:], tab_sc[:].indirect(offs_sb[:]))
 
         w2_raw = [
@@ -240,8 +246,6 @@ def tile_list_milk_bottle_features_kernel(
         for t in range(1, 4):
             pages[t] = held.tile([P, S], F32, name=f"page{t}", tag=("page1", "page2", "sine0_0")[t - 1], align_bytes=(64 if t == 3 else None))
             nc.gpsimd.memset(pages[t][:], 0.0)
-        deal_wgs(2)
-        deal_wgs(3)
         fracs = {1: split_angle(1)}
         for t in range(1, 4):
             if t < 3:
@@ -270,20 +274,20 @@ def tile_list_milk_bottle_features_kernel(
 
         def make_a(h):
             cols = slice(HALF * h, HALF * (h + 1))
-            banks = []
-            for t in range(4):
-                acc = psum.tile([P, HALF], F32, tag=f"a{t}", bufs=1)
-                for a in (1, 0, 2):
-                    nc.tensor.matmul_mx(
-                        out=acc[:],
-                        lhsT=wa_w[:, a, t, :].bitcast(FP4X4),
-                        lhsT_scale=wa_sc[:, a, t, :],
-                        rhs=v_w[a][:, cols].bitcast(FP8X4),
-                        rhs_scale=v_sc[:, a, cols],
-                        start=(a == 1),
-                        stop=(a == PA - 1),
-                    )
-                banks.append(acc)
+            banks = [psum.tile([P, HALF], F32, name="acc", tag=f"a{t}", bufs=1) for t in range(4)]
+            steps = [(a, t) for a in range(PA) for t in range(4)]
+            if h == 1:
+                steps = [(a, t) for t in range(4) for a in range(PA)]
+            for a, t in steps:
+                nc.tensor.matmul_mx(
+                    out=banks[t][:],
+                    lhsT=wa_w[:, a, t, :].bitcast(FP4X4),
+                    lhsT_scale=wa_sc[:, a, t, :],
+                    rhs=v_w[a][:, cols].bitcast(FP8X4),
+                    rhs_scale=v_sc[:, a, cols],
+                    start=(a == 0),
+                    stop=(a == PA - 1),
+                )
             return banks
 
         def make_z(c, banks):

import math
from contextlib import ExitStack

import concourse.mybir as mybir
from concourse.masks import make_identity

K, K2, T, TB, S, L, H, N = 1536, 1024, 4096, 2048, 1024, 512, 512, 1024
FLOPS = 2 * (K * H * S + K2 * H * L + H * N * S)

F32 = mybir.dt.float32
BF16 = mybir.dt.bfloat16
I32 = mybir.dt.int32
U32 = mybir.dt.uint32
U16 = mybir.dt.uint16
U8 = mybir.dt.uint8
FP8X4 = mybir.dt.float8_e4m3fn_x4
FP4X4 = mybir.dt.float4_e2m1fn_x4
ALU = mybir.AluOpType
ACT = mybir.ActivationFunctionType

P = 128
PA = K // 512
PB = K2 // 512
G = N // 512
HALF = 512
CHUNK = 256
ON_SCALAR = ()
Y_ON_SCALAR = ()
ROUNDER = 1.5 * 2.0**23
PER_TURN = 1.0 / (2.0 * math.pi)


def tile_list_milk_bottle_features_kernel(
    tc, tab_words, tab_scales, tab2_words, tab2_scales, offs, offs2, pos1,
    wa_words, wa_scales, wb, wgs, gain, w2, out_0, out_1, out_2,
):
    nc = tc.nc
    with ExitStack() as ctx:
        held = ctx.enter_context(tc.tile_pool(name="held", bufs=1))
        ring = ctx.enter_context(tc.tile_pool(name="ring", bufs=2))
        psum = ctx.enter_context(tc.psum_pool(name="psum", bufs=1))

        def words_of(packed, a):
            return packed[a].rearrange("p n i -> p (n i)").bitcast(I32)

        tab2_sc = held.tile([P, PB, TB], U8, align_bytes=64)
        tab_sc = held.tile([P, T], U8, align_bytes=64)
        wa_sc_raw = held.tile([P, PA, H], U8, align_bytes=64)
        v_sc = held.tile([P, PA, S], U8, align_bytes=64)
        pages = {0: held.tile([P, S], F32, name="page0")}
        nc.vector.memset(tab2_sc[:, 0, :].bitcast(I32), 0)
        nc.gpsimd.memset(tab2_sc[:, 1, :].bitcast(I32), 0)
        nc.vector.memset(tab_sc[:].bitcast(I32), 0)
        nc.vector.memset(wa_sc_raw[:].bitcast(I32), 0)
        nc.vector.memset(pages[0][:], 0.0)
        nc.vector.memset(v_sc[:].bitcast(I32), 0)
        warm = held.tile([P, 2], F32)
        nc.gpsimd.memset(warm[:, 0:1], 0.0)
        nc.scalar.activation(warm[:, 1:2], warm[:, 0:1], ACT.Silu)
        ident = held.tile([P, P], F32)
        make_identity(nc, ident[:])
        gain_sb = held.tile([P, 4], F32)

        offs2_sb = held.tile([P, L // 16], U16)
        offs_sb = held.tile([P, S // 16], U16)
        pos_sb = held.tile([P, L // 16], U16)
        tab2_w = [
            held.tile([P, TB], I32, name=f"tab2_w{a}", tag=("tab2_w0", "tab_w2")[a], align_bytes=64) for a in range(PB)
        ]
        wb_raw = [
            held.tile([P, 4, H], F32, name=f"wb_raw{a}", tag=("raw", "tab_w1")[a], align_bytes=64) for a in range(PB)
        ]
        tab_w = {0: held.tile([P, T], I32, name="tab_w0", tag="tab_w0", align_bytes=64)}
        wgs_sb = held.tile([P, 4, L], F32)
        wa_raw = held.tile([P, PA, 2 * H], U8, align_bytes=64)
        wb_rows = wb.rearrange("(a p i) r -> a p i r", a=PB, i=4)

        wgs_raw = held.tile([P, L], F32)
        nc.sync.dma_start(out=wgs_raw[:], in_=wgs)
        nc.sync.dma_start(offs2_sb[:], offs2)
        for q in range(4):
            nc.sync.dma_start(
                out=tab2_sc[32 * q : 32 * q + 4, :, :].bitcast(I32),
                in_=tab2_scales[:, 4 * q : 4 * q + 4, :].rearrange("a r c -> r a c").bitcast(I32),
            )
        nc.sync.dma_start(offs_sb[:], offs)
        nc.sync.dma_start(out=wb_raw[0][:], in_=wb_rows[0])
        nc.sync.dma_start(
            out=tab_sc[0 : 16 * PA, :].bitcast(I32), in_=tab_scales.rearrange("a q c -> (a q) c").bitcast(I32)
        )
        nc.sync.dma_start(out=wb_raw[1][:], in_=wb_rows[1])
        nc.sync.dma_start(out=wa_raw[:].bitcast(I32), in_=wa_words.rearrange("a p c -> p a c").bitcast(I32))
        for q in range(4):
            nc.sync.dma_start(
                out=wa_sc_raw[32 * q : 32 * q + 4, :, :].bitcast(I32),
                in_=wa_scales[:, 4 * q : 4 * q + 4, :].rearrange("a r c -> r a c").bitcast(I32),
            )
        for a in range(PB):
            nc.sync.dma_start(out=tab2_w[a][:], in_=words_of(tab2_words, a))
        nc.sync.dma_start(pos_sb[:], pos1)
        nc.sync.dma_start(out=gain_sb[:], in_=gain.rearrange("(p t) -> p t", t=4))
        nc.sync.dma_start(out=tab_w[0][:], in_=words_of(tab_words, 0))

        wa_w = held.tile([P, PA, 4, 2 * P], U8, align_bytes=64)
        nc.vector.tensor_copy(out=wa_w[:].bitcast(U16), in_=wa_raw[:].bitcast(U16).rearrange("p a (m t) -> p a t m", t=4))
        wa_sc = held.tile([P, PA, 4, P], U8, align_bytes=64)
        nc.vector.tensor_copy(out=wa_sc[:], in_=wa_sc_raw[:].rearrange("p a (m t) -> p a t m", t=4))

        def quantise_weight(raw, staged, name):
            codes = held.tile([P, 512], U32, name=f"{name}_q", tag=f"{name}_q", align_bytes=64)
            scales = held.tile([P, 512], U8, name=f"{name}_sc", align_bytes=64)
            nc.scalar.copy(
                out=staged[:].rearrange("p t m i -> p m t i"), in_=raw[:].rearrange("p i (m t) -> p m t i", t=4)
            )
            nc.vector.quantize_mx(
                out=codes[:].bitcast(FP8X4), scales=scales[:], in_=staged[:].rearrange("p t m i -> p (t m i)")
            )
            return codes, scales

        wgs_turned = psum.tile([P, 4, P], F32, tag="a0", bufs=1)
        for lb in range(4):
            nc.tensor.transpose(wgs_turned[:, lb, :], wgs_raw[:, P * lb : P * (lb + 1)], ident[:])

        def deal_wgs(t):
            repeated = spread[t]
            rows = wgs_turned[:].rearrange("l b (q t) -> l b t q", t=4)[:, :, t, :]
            nc.scalar.copy(out=repeated, in_=rows.unsqueeze(2).to_broadcast([P, 4, 4, 32]))
            dealt = psum.tile([P, 4, P], F32, tag=f"a{1 + t % 3}", bufs=1)
            for lb in range(4):
                nc.tensor.transpose(dealt[:, lb, :], repeated[:, lb].rearrange("l e q -> l (e q)"), ident[:])
            nc.scalar.copy(out=wgs_sb[:, t, :], in_=dealt[:].rearrange("p b l -> p (b l)"))

        first_spread = held.tile([P, 2, 4, 4, 32], F32)
        spread = {t: first_spread[:, t] for t in range(2)}
        deal_wgs(0)
        deal_wgs(1)
        v2_sc = held.tile([P, PB, L], U8, align_bytes=64)
        for a in range(PB):
            nc.vector.tensor_copy(v2_sc[:, a, :], tab2_sc[:, a, :].indirect(offs2_sb[:]))
        wb_q = []
        for a in range(PB):
            wb_bf = held.tile([P, 4, P, 4], BF16, name=f"wb_bf{a}", align_bytes=64)
            wb_q.append(quantise_weight(wb_raw[a], wb_bf, f"wb{a}"))
        later_spread = held.tile([P, 2, 4, 4, 32], F32, tag="tab_w1", align_bytes=64)
        for t in range(2, 4):
            spread[t] = later_spread[:, t - 2]
            deal_wgs(t)

        v2_w = [held.tile([P, L], U32, name=f"v2_w{a}", align_bytes=64) for a in range(PB)]
        nc.vector.tensor_copy(v2_w[0][:], tab2_w[0][:].bitcast(U32).indirect(offs2_sb[:]))
        for h in range(2):
            nc.vector.tensor_copy(
                v2_w[1][:, 256 * h : 256 * (h + 1)],
                tab2_w[1][:].bitcast(U32).indirect(offs2_sb[:, 16 * h : 16 * (h + 1)]),
            )

        v_sc0 = held.tile([P, S], U8, align_bytes=64)
        nc.vector.tensor_copy(v_sc0[:], tab_sc[:].indirect(offs_sb[:]))

        w2_raw = [
            held.tile([P, 4, 512], F32, name=f"w2_raw{g}", tag=("w2_raw0", "raw")[g], align_bytes=64) for g in range(G)
        ]
        w2_rows = w2.rearrange("(p i) n -> p i n", i=4)
        for g in range(G):
            nc.sync.dma_start(out=w2_raw[g][:], in_=w2_rows[:, :, 512 * g : 512 * (g + 1)])
        for a in range(1, PA):
            tab_w[a] = held.tile([P, T], I32, name=f"tab_w{a}", tag=f"tab_w{a}", align_bytes=64)
            nc.sync.dma_start(out=tab_w[a][:], in_=words_of(tab_words, a))
        for a in range(PA):
            for q in range(4):
                nc.sync.dma_start(
                    out=v_sc[32 * q : 32 * q + 4, a, :].bitcast(I32),
                    in_=v_sc0[16 * a + 4 * q : 16 * a + 4 * q + 4, :].bitcast(I32),
                )

        def reduce_angle(bank, t, l0, width):
            entries = slice(l0, l0 + width)
            x = psum.tile([P, width], F32, tag=bank, bufs=(4 if bank == "y" else 1))
            for a in range(PB):
                codes, scales = wb_q[a]
                nc.tensor.matmul_mx(
                    out=x[:],
                    lhsT=codes[:, P * t : P * (t + 1)].bitcast(FP8X4),
                    lhsT_scale=scales[:, P * t : P * (t + 1)],
                    rhs=v2_w[a][:, entries].bitcast(FP8X4),
                    rhs_scale=v2_sc[:, a, entries],
                    start=(a == 0),
                    stop=(a == PB - 1),
                )
            shifted = ring.tile([P, width], U32)
            nc.scalar.activation(shifted[:], x[:], ACT.Copy, bias=ROUNDER, scale=PER_TURN)
            whole = held.tile([P, width], F32, tag=f"page{1 + l0 // width}")
            frac = held.tile([P, width], F32, tag=f"first{l0}")
            nc.scalar.activation(whole[:], shifted[:], ACT.Copy, bias=-ROUNDER)
            nc.vector.scalar_tensor_tensor(frac[:], x[:], PER_TURN, whole[:], ALU.mult, ALU.subtract)
            return frac

        def split_angle(t):
            x = psum.tile([P, 4, P], F32, tag="y", bufs=4)
            for lb in range(4):
                entries = slice(P * lb, P * (lb + 1))
                for a in range(PB):
                    codes, scales = wb_q[a]
                    nc.tensor.matmul_mx(
                        out=x[:, lb, :],
                        lhsT=v2_w[a][:, entries].bitcast(FP8X4),
                        lhsT_scale=v2_sc[:, a, entries],
                        rhs=codes[:, P * t : P * (t + 1)].bitcast(FP8X4),
                        rhs_scale=scales[:, P * t : P * (t + 1)],
                        start=(a == 0),
                        stop=(a == PB - 1),
                    )
            shifted = held.tile([P, 4, P], U32, tag=("first0", "first256")[t % 2 - 1])
            nc.scalar.activation(shifted[:], x[:], ACT.Copy, bias=ROUNDER, scale=PER_TURN)
            if t < 3:
                turns = ring.tile([P, 4, P], F32)
                whole = ring.tile([P, 4, P], F32)
            else:
                turns = held.tile([P, 4, P], F32, tag="w2_bf0", align_bytes=64)
                whole = held.tile([P, 4, P], F32, tag="w2_bf1", align_bytes=64)
            nc.scalar.activation(turns[:], x[:], ACT.Copy, scale=PER_TURN)
            nc.scalar.activation(whole[:], shifted[:], ACT.Copy, bias=ROUNDER, scale=-1.0)
            frac = psum.tile([P, L], F32, tag=f"a{t}", bufs=1)
            for lb in range(4):
                nc.tensor.matmul(
                    frac[:, P * lb : P * (lb + 1)], turns[:, lb, :], ident[:], start=(lb == 0), stop=False, is_transpose=True
                )
            for lb in range(4):
                nc.tensor.matmul(
                    frac[:, P * lb : P * (lb + 1)], whole[:, lb, :], ident[:], start=False, stop=(lb == 3), is_transpose=True
                )
            return frac

        def place(t, frac, l0, width):
            b = held.tile([P, width], F32, tag=f"sine{t}_{l0}", align_bytes=64)
            nc.scalar.activation(b[:], frac[:], ACT.Sin, scale=2.0 * math.pi)
            nc.vector.tensor_tensor(
                pages[t][:].indirect(pos_sb[:, l0 // 16 : (l0 + width) // 16]),
                b[:],
                wgs_sb[:, t, l0 : l0 + width],
                ALU.mult,
            )

        for h in range(2):
            place(0, reduce_angle("y", 0, h * L // 2, L // 2), h * L // 2, L // 2)
        for t in range(1, 4):
            pages[t] = held.tile([P, S], F32, name=f"page{t}", tag=("page1", "page2", "sine0_0")[t - 1], align_bytes=(64 if t == 3 else None))
            nc.gpsimd.memset(pages[t][:], 0.0)
        fracs = {1: split_angle(1)}
        for t in range(1, 4):
            if t < 3:
                fracs[t + 1] = split_angle(t + 1)
            place(t, fracs[t], 0, L)

        v_w = [held.tile([P, S], U32, name=f"v_w{a}", tag=("sine0_256", "sine2_0", "sine3_0")[a], align_bytes=64) for a in range(PA)]
        for a in range(PA - 1):
            nc.vector.tensor_copy(v_w[a][:], tab_w[a][:].bitcast(U32).indirect(offs_sb[:]))

        w2_q = []
        for g in range(G):
            w2_bf = held.tile([P, 4, P, 4], BF16, tag=f"w2_bf{g}", align_bytes=64)
            w2_q.append(quantise_weight(w2_raw[g], w2_bf, f"w2{g}"))

        y_q = held.tile([P, G, S], U32, align_bytes=64)
        y_sc = held.tile([P, G, S], U8, align_bytes=64)
        y_rows = out_0.rearrange("(g p t) j -> g p t j", g=G, t=4)
        y_words = out_1.rearrange("g p m i -> p g (m i)").bitcast(I32)

        def gather_last(h):
            nc.vector.tensor_copy(
                v_w[PA - 1][:, HALF * h : HALF * (h + 1)],
                tab_w[PA - 1][:].bitcast(U32).indirect(offs_sb[:, 32 * h : 32 * (h + 1)]),
            )

        def make_a(h):
            cols = slice(HALF * h, HALF * (h + 1))
            banks = [psum.tile([P, HALF], F32, name="acc", tag=f"a{t}", bufs=1) for t in range(4)]
            steps = [(a, t) for a in range(PA) for t in range(4)]
            if h == 1:
                steps = [(a, t) for t in range(4) for a in range(PA)]
            for a, t in steps:
                nc.tensor.matmul_mx(
                    out=banks[t][:],
                    lhsT=wa_w[:, a, t, :].bitcast(FP4X4),
                    lhsT_scale=wa_sc[:, a, t, :],
                    rhs=v_w[a][:, cols].bitcast(FP8X4),
                    rhs_scale=v_sc[:, a, cols],
                    start=(a == 0),
                    stop=(a == PA - 1),
                )
            return banks

        def make_z(c, banks):
            cols = slice(CHUNK * c, CHUNK * (c + 1))
            z_rows = ring.tile([P, 4, CHUNK], BF16, align_bytes=64)
            for t in range(4):
                acc = banks[t][:, CHUNK * (c % 2) : CHUNK * (c % 2 + 1)]
                s = ring.tile([P, CHUNK], F32, bufs=4)
                nc.vector.tensor_tensor(s[:], acc, pages[t][:, cols], ALU.add)
                a_gain = ring.tile([P, CHUNK], F32, bufs=4)
                nc.scalar.activation(a_gain[:], acc, ACT.Copy, scale=gain_sb[:, t : t + 1])
                th = ring.tile([P, CHUNK], F32, bufs=4)
                nc.scalar.activation(th[:], s[:], ACT.Tanh)
                nc.vector.scalar_tensor_tensor(
                    z_rows[:, t, :], th[:], gain_sb[:, t : t + 1], a_gain[:], ALU.mult, ALU.add
                )
            z_bf = ring.tile([P, CHUNK, 4], BF16, align_bytes=64)
            interleave = nc.scalar.copy if c in ON_SCALAR else nc.vector.tensor_copy
            interleave(
                out=z_bf[:].rearrange("p (c e) t -> p c t e", e=4),
                in_=z_rows[:].rearrange("p t (c e) -> p c t e", e=4),
            )
            z_q = ring.tile([P, CHUNK], U32, bufs=4, align_bytes=64)
            z_sc = ring.tile([P, CHUNK], U8, bufs=4, align_bytes=64)
            nc.vector.quantize_mx(out=z_q[:].bitcast(FP8X4), scales=z_sc[:], in_=z_bf[:].rearrange("p j t -> p (j t)"))
            return z_q, z_sc

        def make_y(c, z_q, z_sc):
            cols = slice(CHUNK * c, CHUNK * (c + 1))
            y_both = held.tile([P, G, 4, CHUNK], F32, tag=("tab_w0", "tab_w1", "raw", "w2_raw0")[c], align_bytes=64)
            for g in range(G):
                codes, scales = w2_q[g]
                y_sb = y_both[:, g]
                for tt in range(2):
                    bank = psum.tile([P, 2, CHUNK], F32, tag="y", bufs=4)
                    for e in range(2):
                        t = 2 * tt + e
                        nc.tensor.matmul_mx(
                            out=bank[:, e, :],
                            lhsT=codes[:, P * t : P * (t + 1)].bitcast(FP8X4),
                            lhsT_scale=scales[:, P * t : P * (t + 1)],
                            rhs=z_q[:].bitcast(FP8X4),
                            rhs_scale=z_sc[:],
                            start=True,
                            stop=True,
                        )
                    nc.scalar.copy(out=y_sb[:, 2 * tt : 2 * tt + 2, :], in_=bank[:])
                nc.sync.dma_start(out=y_rows[g][:, :, cols], in_=y_sb)
            return y_both

        def make_planes(c, y_both):
            cols = slice(CHUNK * c, CHUNK * (c + 1))
            for g in range(G):
                y_sb = y_both[:, g]
                y_bf = ring.tile([P, CHUNK, 4], BF16, bufs=3, align_bytes=64)
                interleave = nc.scalar.copy if (c, g) in Y_ON_SCALAR else nc.vector.tensor_copy
                interleave(
                    out=y_bf[:].rearrange("p (c e) t -> p c t e", e=4),
                    in_=y_sb.rearrange("p t (c e) -> p c t e", e=4),
                )
                nc.vector.quantize_mx(
                    out=y_q[:, g, cols].bitcast(FP8X4), scales=y_sc[:, g, cols], in_=y_bf[:].rearrange("p j t -> p (j t)")
                )
            nc.sync.dma_start(out=y_words[:, :, cols], in_=y_q[:, :, cols].bitcast(I32))

        gather_last(0)
        banks = {0: make_a(0)}
        z = {}
        y = {}
        z[0] = make_z(0, banks[0])
        gather_last(1)
        z[1] = make_z(1, banks[0])
        banks[1] = make_a(1)
        y[0] = make_y(0, *z[0])
        z[2] = make_z(2, banks[1])
        y[1] = make_y(1, *z[1])
        z[3] = make_z(3, banks[1])
        y[2] = make_y(2, *z[2])
        y[3] = make_y(3, *z[3])
        make_planes(0, y[0])
        make_planes(1, y[1])
        make_planes(2, y[2])
        make_planes(3, y[3])

        for q in range(4):
            nc.sync.dma_start(
                out=out_2[:, 4 * q : 4 * q + 4, :].rearrange("g r m -> r g m").bitcast(I32),
                in_=y_sc[32 * q : 32 * q + 4, :, :].bitcast(I32),
            )
